import numpy as np
import ml_dtypes


def mxq(x, axis, fmt="e4m3"):
    dtype, down = {"e4m3": (ml_dtypes.float8_e4m3fn, 7), "e5m2": (ml_dtypes.float8_e5m2, 14)}[fmt]
    v = np.moveaxis(np.asarray(x, np.float32).astype(ml_dtypes.bfloat16).astype(np.float64), axis, -1)
    blocks = v.reshape(v.shape[:-1] + (-1, 32))
    amax = np.abs(blocks).max(-1, keepdims=True)
    byte = np.maximum(np.where(amax > 0, np.frexp(amax)[1] - 1 + 127, 0) - down, 1)
    scale = np.exp2(byte - 127.0)
    codes = (blocks / scale).astype(np.float32).astype(dtype).astype(np.float64)
    return np.moveaxis((codes * scale).reshape(v.shape), -1, axis)


WIDE = False


def mx_kscale(k):
    if not WIDE:
        return np.ones(k)
    levels = np.array([10, -10, 5, -5, 0])
    if k % 512:
        return np.exp2(np.random.permutation(np.resize(levels, k // 32))).repeat(32)
    a = np.empty((k // 512, 16))
    for p in range(k // 512):
        a[p, :8] = np.random.permutation(np.resize(levels, 8))
        for g in range(8):
            far = levels[np.abs(levels - a[p, g]) >= 10]
            a[p, g + 8] = far[np.random.randint(len(far))]
    return np.exp2(a.ravel()).repeat(32)


def f64(x):
    return np.asarray(x).astype(np.float64)


def striped(idx):
    return np.tile(idx.reshape(-1, 16).T, (8, 1)).astype(np.uint16)


def unstriped(offs):
    return offs[:16].T.reshape(-1).astype(np.int64)


E2M1 = np.array([0.0, 0.5, 1.0, 1.5, 2.0, 3.0, 4.0, 6.0, -0.0, -0.5, -1.0, -1.5, -2.0, -3.0, -4.0, -6.0])


def pack_weight(w, fmt):
    k, n = w.shape
    w = f64(np.asarray(w, np.float32).astype(ml_dtypes.bfloat16)).reshape(k // 32, 32, n)
    amax = np.abs(w).max(1)
    if fmt == "e4m3":
        byte = np.frexp(amax)[1] - 1 + 127 - 7
    else:
        mant, ex = np.frexp(amax / 6.0)
        byte = np.where(mant > 0.5, ex, ex - 1) + 127
    byte = np.clip(np.where(amax > 0, byte, 1), 1, 254)
    scaled = (w * np.exp2(127.0 - byte)[:, None, :]).reshape(k, n).astype(np.float32)
    by_word = np.ascontiguousarray(scaled.reshape(k // 512, 128, 4, n).transpose(0, 1, 3, 2))
    if fmt == "e4m3":
        words = by_word.astype(ml_dtypes.float8_e4m3fn).view(np.uint8)
    else:
        c = by_word.astype(ml_dtypes.float4_e2m1fn).view(np.uint8) & 0xF
        words = (c[..., 0::2] | (c[..., 1::2] << 4)).reshape(k // 512, 128, 2 * n)
    return np.ascontiguousarray(words), np.ascontiguousarray(byte.astype(np.uint8).reshape(k // 512, 16, n))


def unpack_weight(words, scales, fmt):
    g, _, n = scales.shape
    words = np.ascontiguousarray(words).reshape(g, 128, n, -1)
    if fmt == "e4m3":
        vals = words.view(ml_dtypes.float8_e4m3fn).astype(np.float64)
    else:
        nib = np.empty((g, 128, n, 4), np.uint8)
        nib[..., 0::2] = words & 0xF
        nib[..., 1::2] = words >> 4
        vals = E2M1[nib]
    vals = vals * np.repeat(np.exp2(scales.astype(np.float64) - 127.0), 8, axis=1)[..., None]
    return vals.transpose(0, 1, 3, 2).reshape(g * 512, n)


def planes(y):
    n, m = y.shape
    v = y.astype(np.float32).astype(ml_dtypes.bfloat16).astype(np.float64).reshape(n // 32, 32, m)
    top = np.abs(v).max(1)
    byte = np.clip(np.where(top > 0, np.frexp(top)[1] - 1 + 127 - 7, 1), 1, 254)
    codes = (v * np.exp2(127.0 - byte)[:, None, :]).reshape(n, m).astype(np.float32).astype(ml_dtypes.float8_e4m3fn).view(np.uint8)
    words = codes.reshape(n // 512, 128, 4, m).transpose(0, 1, 3, 2)
    return np.ascontiguousarray(words), np.ascontiguousarray(byte.astype(np.uint8).reshape(n // 512, 16, m))


K, T, G, C1, E, C2, H = 1024, 1024, 4, 256, 8, 128, 512
N = 512


def by_expert(wq, xq, E, C):
    return np.concatenate([wq[e].T @ xq[:, e * C:(e + 1) * C] for e in range(E)], axis=1)


def setup_inputs():
    n = np.random.standard_normal
    s = mx_kscale(K)
    u = mx_kscale(H)
    slots1 = np.random.permutation(T)
    slots2 = np.concatenate([q * C1 + np.random.permutation(C1) for q in range(G)])
    x = pack_weight(n((K, T)) * s[:, None], "e4m3")
    wg = [pack_weight(m, "e2m1") for m in n((G, K, H)) / np.sqrt(K) / s[None, :, None] * u]
    we = [pack_weight(m, "e4m3") for m in n((E, H, N)) / np.sqrt(H) / u[None, :, None]]
    return {
        "x_words": x[0],
        "x_scales": x[1],
        "wg_words": np.stack([m[0] for m in wg]),
        "wg_scales": np.stack([m[1] for m in wg]),
        "we_words": np.stack([m[0] for m in we]),
        "we_scales": np.stack([m[1] for m in we]),
        "gate": (np.tile(np.random.uniform(0.2, 1.0, T), (128, 1))).astype(np.float32),
        "offs": striped(slots1),
        "offs2": striped(slots2),
        "dst": striped(slots1[slots2]),
    }


def reference(x_words, x_scales, wg_words, wg_scales, we_words, we_scales, gate, offs, offs2, dst):
    wg = np.stack([unpack_weight(wg_words[e], wg_scales[e], "e2m1") for e in range(G)])
    we = np.stack([unpack_weight(we_words[e], we_scales[e], "e4m3") for e in range(E)])
    idx, idx2 = unstriped(offs), unstriped(offs2)
    xq = unpack_weight(x_words, x_scales, "e4m3")[:, idx]
    a = by_expert(wg, xq, G, C1)
    y = by_expert(we, mxq(a[:, idx2], 0, "e4m3"), E, C2)
    out = np.zeros((N, T))
    out[:, unstriped(dst)] = f64(gate[:1]) * y
    out_0 = out
    return (out_0,) + planes(out_0)

@@ -1,0 +1,291 @@
+from contextlib import ExitStack
+
+import concourse.mybir as mybir
+from concourse.masks import make_identity
+
+K, T, G, C1, E, C2, H, N = 1024, 1024, 4, 256, 8, 128, 512, 512
+FLOPS = 2 * K * H * T + 2 * H * N * T
+
+F32 = mybir.dt.float32
+BF16 = mybir.dt.bfloat16
+I32 = mybir.dt.int32
+U32 = mybir.dt.uint32
+U16 = mybir.dt.uint16
+U8 = mybir.dt.uint8
+FP8X4 = mybir.dt.float8_e4m3fn_x4
+FP4X4 = mybir.dt.float4_e2m1fn_x4
+COPY = mybir.ActivationFunctionType.Copy
+
+P = 128
+PASSES = 2
+EPG = 2
+LIST_COLS = 16
+VECTOR_GROUPS = (0, 1)
+FIRST_BANKS = ((0, 1, 2), (3, 4, 5), (3, 4, 2), (6, 7, 4))
+TURNED_BANKS = (1, 1, 1, 2)
+BANK = 2048
+PLACE_GROUPED = {0: 0, 1: 2048, 2: 4096}
+PLACE_Y_ROWS = {1: 4096}
+PLACE_Y_SLOTS = {0: 6144, 1: 10240}
+PLACE_CODES = {2: 6144, 3: 10240}
+PLACE_WORDS = {(3, 0, 0): 512, (3, 0, 1): 2048, (0, 0, 0): 40960, (0, 0, 1): 43008, (2, 0, 0): 40960, (2, 0, 1): 43008}
+PLACE_SCALES = {(0, 0, 0): 45056, (0, 0, 1): 45312, (2, 0, 0): 45056, (2, 0, 1): 45312, (3, 0, 0): 0, (3, 0, 1): 256}
+PLACE_LATE_LOADS = 14848
+SECOND_BANKS = ((0, 1, 6, 7), (6, 7, 0, 1), (4, 5, 0, 1), (2, 3, 6, 7))
+
+
+def tile_moe_hie_none_kernel(
+    tc, x_words, x_scales, wg_words, wg_scales, we_words, we_scales, gate, offs, offs2, dst, out_0, out_1, out_2
+):
+    nc = tc.nc
+    with ExitStack() as ctx:
+        keep = ctx.enter_context(tc.tile_pool(name="keep", bufs=1))
+        ring = ctx.enter_context(tc.tile_pool(name="ring", bufs=2))
+        placed = ctx.enter_context(tc.tile_pool(name="placed", bufs=1))
+        psum = ctx.enter_context(tc.psum_pool(name="psum", bufs=1))
+
+        def sbuf_tile(shape, dtype, name, place=None):
+            if place is None:
+                return keep.tile(shape, dtype, name=name, align_bytes=64)
+            return placed.tile(shape, dtype, name=name, offset=place, align_bytes=64)
+
+        def load_scale_rows(queue, plane, rows, blocks):
+            by_row = rows.bitcast(I32).rearrange("s (q r) c -> r q s c", r=4)
+            for r in range(4):
+                queue.dma_start(
+                    out=plane[r:P:32, :].bitcast(I32).rearrange("q (s c) -> q s c", s=blocks), in_=by_row[r]
+                )
+
+        x_plane = keep.tile([P, PASSES * T], U8, name="x_plane", align_bytes=64)
+        wg_plane = keep.tile([P, G * PASSES * H], U8, name="wg_plane", align_bytes=64)
+        we_plane = keep.tile([P, E * N], U8, name="we_plane", align_bytes=64)
+        nc.vector.memset(x_plane[:].bitcast(I32), 0)
+        nc.vector.memset(wg_plane[:].bitcast(I32), 0)
+
+        offs_sb = keep.tile([P, T // 16], U16, name="offs_sb")
+        nc.sync.dma_start(offs_sb[:], offs)
+        offs2_sb = keep.tile([P, T // 16], U16, name="offs2_sb")
+        nc.sync.dma_start(offs2_sb[:], offs2)
+        dst_sb = keep.tile([P, T // 16], U16, name="dst_sb")
+        nc.sync.dma_start(dst_sb[:], dst)
+        load_scale_rows(nc.sync, x_plane, x_scales, PASSES)
+        x_sb = keep.tile([P, PASSES * T], I32, name="x_sb", align_bytes=64)
+        nc.sync.dma_start(
+            out=x_sb[:].rearrange("p (s t) -> p s t", s=PASSES),
+            in_=x_words.rearrange("s p t d -> p s (t d)").bitcast(I32),
+        )
+
+        wg_first = keep.tile([P, PASSES * 2 * H], U8, name="wg_first", align_bytes=64)
+        ident_src = sbuf_tile([P, P], F32, "ident_src", PLACE_LATE_LOADS)
+        make_identity(nc, ident_src[:])
+        nc.gpsimd.memset(we_plane[:].bitcast(I32), 0)
+        ident_f32 = keep.tile([P, P], F32, name="ident_f32")
+        ident_bf16 = keep.tile([P, P], BF16, name="ident_bf16")
+        nc.vector.tensor_copy(ident_f32[:], ident_src[:])
+        nc.vector.tensor_copy(ident_bf16[:], ident_src[:])
+        wg_bytes, we_bytes = PASSES * 2 * H, EPG * 4 * N
+        weights = sbuf_tile([P, (G - 1) * wg_bytes + G * we_bytes], U8, "weights", PLACE_LATE_LOADS + 64)
+        wg_sb = [wg_first[:]] + [weights[:, g * wg_bytes : (g + 1) * wg_bytes] for g in range(G - 1)]
+        we_first = (G - 1) * wg_bytes
+        we_sb = [weights[:, we_first + g * we_bytes : we_first + (g + 1) * we_bytes] for g in range(G)]
+
+        def load_wg(g):
+            nc.sync.dma_start(
+                out=wg_sb[g].bitcast(I32).rearrange("p (s c) -> p s c", s=PASSES),
+                in_=wg_words[g].bitcast(I32).rearrange("s p c -> p s c"),
+            )
+
+        def load_we(g):
+            rows = we_words[EPG * g : EPG * (g + 1), 0].rearrange("e p n d -> e p (n d)").bitcast(I32)
+            nc.sync.dma_start(
+                out=we_sb[g].bitcast(I32).rearrange("p (e n) -> p e n", e=EPG), in_=rows.rearrange("e p n -> p e n")
+            )
+
+        load_wg(0)
+        load_scale_rows(nc.sync, wg_plane, wg_scales.rearrange("f s b c -> (f s) b c"), G * PASSES)
+        load_wg(1)
+        gate_rows = sbuf_tile([P, C2], F32, "gate_rows", PLACE_LATE_LOADS + 64 - 4 * C2)
+        nc.sync.dma_start(out=gate_rows[:], in_=gate[: P // E, :].rearrange("r (e c) -> (r e) c", e=E))
+        load_wg(2)
+        load_we(0)
+        load_scale_rows(nc.sync, we_plane, we_scales.rearrange("e s b c -> (e s) b c"), E)
+        load_we(1)
+        load_wg(3)
+        load_we(2)
+        load_we(3)
+        warm = keep.tile([P, 1], F32, name="warm")
+        nc.scalar.activation(warm[:], ident_f32[:, 0:1], COPY)
+
+        a_win = []
+        for g in range(G):
+            if g in VECTOR_GROUPS:
+                planes, dtype, words = 2, F32, C1
+            else:
+                planes, dtype, words = 4, BF16, C1 // 2
+            tail = C1 if g == 0 else 0
+            win = keep.tile([P, g * C1 + planes * C1 + tail], dtype, name=f"a_win{g}", align_bytes=64)
+            if g == 0:
+                nc.vector.memset(win[:, planes * C1 :].bitcast(I32), 0)
+            else:
+                nc.vector.memset(win[:, : g * C1].bitcast(I32), 0)
+            a_win.append(win)
+
+        y_win = [keep.tile([P, T], F32, name=f"y_win{t}") for t in range(4)]
+        pairs = [keep.tile([P, 2, T // 2, 2], BF16, name=f"pairs{h}", align_bytes=64) for h in range(2)]
+        out_rows = out_0.rearrange("(p t) c -> p t c", t=4)
+
+        def list_slice(tile, first, count):
+            return tile[:, first // 16 : (first + count) // 16]
+
+        def gather_tokens(g):
+            pieces = 2 if g == 0 else 1
+            count = C1 // pieces
+            words, scales = [], []
+            for h in range(pieces):
+                entries = list_slice(offs_sb, g * C1 + h * count, count)
+                for s in range(PASSES):
+                    sc = sbuf_tile([P, count], U8, f"xg_scales{g}_{h}_{s}", PLACE_SCALES.get((g, h, s)))
+                    nc.vector.tensor_copy(sc[:], x_plane[:, s * T : (s + 1) * T].indirect(entries))
+                    w = sbuf_tile([P, count], U32, f"xg_words{g}_{h}_{s}", PLACE_WORDS.get((g, h, s)))
+                    nc.vector.tensor_copy(w[:], x_sb[:, s * T : (s + 1) * T].bitcast(U32).indirect(entries))
+                    for first in range(0, count, P):
+                        scales.append(sc[:, first : first + P])
+                        words.append(w[:, first : first + P])
+            order = [0, 1, 2, 3] if pieces == 2 else [0, 2, 1, 3]
+            return [words[i] for i in order], [scales[i] for i in order]
+
+        def first_layer(g, words, scales):
+            on_vector = g in VECTOR_GROUPS
+            planes = 2 if on_vector else 4
+            turned_banks = psum.tile(
+                [P, TURNED_BANKS[g] * planes, C1], F32 if on_vector else BF16, name=f"turned{g}", offset=BANK * FIRST_BANKS[g][2]
+            )
+            turned = turned_banks[:, :planes, :]
+            for h in range(2):
+                cols = slice(h * P, (h + 1) * P)
+                acc = psum.tile([P, H], F32, name=f"acc1_{g}_{h}", offset=BANK * FIRST_BANKS[g][h])
+                for s in range(PASSES):
+                    first = (g * PASSES + s) * H
+                    nc.tensor.matmul_mx(
+                        out=acc[:],
+                        lhsT=words[h * PASSES + s].bitcast(FP8X4),
+                        lhsT_scale=scales[h * PASSES + s],
+                        rhs=wg_sb[g][:, s * 2 * H : (s + 1) * 2 * H].bitcast(FP4X4),
+                        rhs_scale=wg_plane[:, first : first + H],
+                        start=(s == 0),
+                        stop=(s == PASSES - 1),
+                    )
+                a_rows = ring.tile([P, H], BF16, name="a_rows", align_bytes=64)
+                if on_vector:
+                    nc.scalar.copy(
+                        a_rows[:].rearrange("p (u m e) -> p u m e", u=2, e=2),
+                        acc[:].rearrange("p (m u e) -> p u m e", u=2, e=2),
+                    )
+                    for u in range(2):
+                        nc.tensor.transpose(turned[:, u, cols], a_rows[:].bitcast(F32)[:, u * P : (u + 1) * P], ident_f32[:])
+                else:
+                    nc.scalar.copy(
+                        a_rows[:].rearrange("p (t m) -> p t m", t=4), acc[:].rearrange("p (m t) -> p t m", t=4)
+                    )
+                    for t in range(4):
+                        nc.tensor.transpose(turned[:, t, cols], a_rows[:, t * P : (t + 1) * P], ident_bf16[:])
+            nc.scalar.copy(a_win[g][:, g * C1 : (g + planes) * C1], turned.rearrange("p t c -> p (t c)"))
+
+        def second_gather(g):
+            width = max(g + 1, 2) * C1
+            entries = list_slice(offs2_sb, g * C1, C1)
+            grouped = sbuf_tile([P, C1 * 4], BF16, f"a_grouped{g}", PLACE_GROUPED.get(g))
+            if g in VECTOR_GROUPS:
+                target = grouped[:].bitcast(U32).rearrange("p (c u) -> p c u", u=2)
+                for u in range(2):
+                    window = a_win[g][:, u * C1 : u * C1 + width].bitcast(U32)
+                    nc.vector.tensor_copy(target[:, :, u], window.indirect(entries))
+            else:
+                target = grouped[:].rearrange("p (c t) -> p c t", t=4)
+                for t in range(4):
+                    window = a_win[g][:, t * C1 : t * C1 + width]
+                    nc.scalar.activation(target[:, :, t], window.indirect(entries), COPY)
+            return grouped
+
+        def quantise(g, grouped):
+            codes = sbuf_tile([P, C1], U32, f"a_codes{g}", PLACE_CODES.get(g))
+            scales = keep.tile([P, C1], U8, name=f"a_scales{g}", align_bytes=64)
+            nc.vector.quantize_mx(out=codes[:].bitcast(FP8X4), scales=scales[:], in_=grouped[:])
+            return codes, scales
+
+        def second_layer(g, codes, scales):
+            y_slots = sbuf_tile([P, 4, C1], F32, f"y_slots{g}", PLACE_Y_SLOTS.get(g))
+            for j in range(EPG):
+                e = g * EPG + j
+                cols = slice(j * C2, (j + 1) * C2)
+                acc = psum.tile([P, N], F32, name=f"acc2_{e}", offset=BANK * SECOND_BANKS[g][j])
+                nc.tensor.matmul_mx(
+                    out=acc[:],
+                    lhsT=codes[:, cols].bitcast(FP8X4),
+                    lhsT_scale=scales[:, cols],
+                    rhs=we_sb[g][:, j * 4 * N : (j + 1) * 4 * N].bitcast(FP8X4),
+                    rhs_scale=we_plane[:, e * N : (e + 1) * N],
+                    start=True,
+                    stop=True,
+                )
+                y_rows = sbuf_tile([P, 4, P], F32, f"y_rows{e}", PLACE_Y_ROWS.get(e))
+                nc.scalar.activation(
+                    y_rows[:], acc[:].rearrange("p (m t) -> p t m", t=4), COPY, scale=gate_col[:, e : e + 1]
+                )
+                back = psum.tile([P, 4, C2], F32, name=f"back{e}", offset=BANK * SECOND_BANKS[g][EPG + j])
+                for t in range(4):
+                    nc.tensor.transpose(back[:, t, :], y_rows[:, t, :], ident_f32[:])
+                nc.scalar.copy(y_slots[:, :, cols], back[:])
+            return y_slots
+
+        def scatter(g, y_slots):
+            entries = list_slice(dst_sb, g * C1, C1)
+            for t in range(4):
+                nc.vector.tensor_copy(y_win[t][:].indirect(entries), y_slots[:, t, :])
+
+        tokens = [gather_tokens(g) for g in range(2)]
+        first_layer(0, *tokens[0])
+        tokens.append(gather_tokens(2))
+        first_layer(1, *tokens[1])
+        gate_turned = psum.tile([P, P], F32, name="gate_turned", offset=BANK * 7)
+        nc.tensor.transpose(gate_turned[:], gate_rows[:], ident_f32[:])
+        gate_col = keep.tile([P, E], F32, name="gate_col")
+        nc.scalar.copy(gate_col[:], gate_turned[:, :E])
+        quantised0 = quantise(0, second_gather(0))
+        y0 = second_layer(0, *quantised0)
+        first_layer(2, *tokens[2])
+        quantised1 = quantise(1, second_gather(1))
+        tokens3 = gather_tokens(3)
+        grouped2 = second_gather(2)
+        y1 = second_layer(1, *quantised1)
+        first_layer(3, *tokens3)
+        scatter(0, y0)
+        quantised2 = quantise(2, grouped2)
+        grouped3 = second_gather(3)
+        y2 = second_layer(2, *quantised2)
+        scatter(1, y1)
+        quantised3 = quantise(3, grouped3)
+        y3 = second_layer(3, *quantised3)
+        scatter(2, y2)
+        scatter(3, y3)
+
+        halves = [slice(0, T // 2), slice(T // 2, T)]
+        for t in range(4):
+            nc.sync.dma_start(out=out_rows[:, t, :], in_=y_win[t][:])
+            for h, cols in enumerate(halves):
+                nc.scalar.copy(pairs[h][:, t // 2, :, t % 2], y_win[t][:, cols])
+        out_codes = keep.tile([P, T], I32, name="out_codes", align_bytes=64)
+        out_plane = keep.tile([P, T], U8, name="out_plane", align_bytes=64)
+        code_rows = out_1[0].rearrange("p c d -> p (c d)").bitcast(I32)
+        for h, cols in enumerate(halves):
+            pair_words = pairs[h][:].rearrange("p u c e -> p u (c e)").bitcast(I32)
+            grouped = ring.tile([P, 2 * T], BF16, name="y_grouped", align_bytes=64)
+            nc.vector.tensor_copy(
+                grouped[:].bitcast(I32).rearrange("p (c u) -> p c u", u=2),
+                pair_words.rearrange("p u c -> p c u"),
+            )
+            nc.vector.quantize_mx(out=out_codes[:, cols].bitcast(FP8X4), scales=out_plane[:, cols], in_=grouped[:])
+            nc.sync.dma_start(out=code_rows[:, cols], in_=out_codes[:, cols])
+        scale_rows = out_2[0].bitcast(I32).rearrange("(q r) c -> r q c", r=4)
+        for r in range(4):
+            nc.scalar.dma_start(out=scale_rows[r], in_=out_plane[r:P:32, :].bitcast(I32))

@@ -20,18 +20,18 @@ P = 128
 PASSES = 2
 EPG = 2
 LIST_COLS = 16
-VECTOR_GROUPS = (0, 1)
-FIRST_BANKS = ((0, 1, 2), (3, 4, 5), (3, 4, 2), (6, 7, 4))
+VECTOR_GROUPS = (0, 1, 2)
+FIRST_BANKS = ((0, 1, 4), (2, 3, 5), (0, 1, 6), (0, 1, 2))
 TURNED_BANKS = (1, 1, 1, 2)
 BANK = 2048
-PLACE_GROUPED = {0: 0, 1: 2048, 2: 4096}
-PLACE_Y_ROWS = {1: 4096}
-PLACE_Y_SLOTS = {0: 6144, 1: 10240}
-PLACE_CODES = {2: 6144, 3: 10240}
-PLACE_WORDS = {(3, 0, 0): 512, (3, 0, 1): 2048, (0, 0, 0): 40960, (0, 0, 1): 43008, (2, 0, 0): 40960, (2, 0, 1): 43008}
-PLACE_SCALES = {(0, 0, 0): 45056, (0, 0, 1): 45312, (2, 0, 0): 45056, (2, 0, 1): 45312, (3, 0, 0): 0, (3, 0, 1): 256}
+PLACE_GROUPED = {}
+PLACE_Y_ROWS = {}
+PLACE_Y_SLOTS = {0: 6144}
+PLACE_CODES = {3: 6144}
+PLACE_WORDS = {(0, 0, 0): 768, (2, 0, 0): 0, (3, 0, 0): 1024, (0, 0, 1): 2816, (2, 0, 1): 2048, (3, 0, 1): 3072}
+PLACE_SCALES = {(0, 0, 0): 4288, (2, 0, 0): 4096, (3, 0, 0): 4352, (0, 0, 1): 4800, (2, 0, 1): 4608, (3, 0, 1): 4864}
 PLACE_LATE_LOADS = 14848
-SECOND_BANKS = ((0, 1, 6, 7), (6, 7, 0, 1), (4, 5, 0, 1), (2, 3, 6, 7))
+SECOND_BANKS = ((1, 6, 4, 5), (4, 5, 0, 1), (2, 3, 4, 5), (4, 5, 6, 7))
 
 
 def tile_moe_hie_none_kernel(
@@ -69,11 +69,10 @@ def tile_moe_hie_none_kernel(
         dst_sb = keep.tile([P, T // 16], U16, name="dst_sb")
         nc.sync.dma_start(dst_sb[:], dst)
         load_scale_rows(nc.sync, x_plane, x_scales, PASSES)
-        x_sb = keep.tile([P, PASSES * T], I32, name="x_sb", align_bytes=64)
-        nc.sync.dma_start(
-            out=x_sb[:].rearrange("p (s t) -> p s t", s=PASSES),
-            in_=x_words.rearrange("s p t d -> p s (t d)").bitcast(I32),
-        )
+        x_sb = []
+        for s in range(PASSES):
+            x_sb.append(keep.tile([P, T], I32, name=f"x_sb{s}", align_bytes=64))
+            nc.sync.dma_start(out=x_sb[s][:], in_=x_words[s].rearrange("p t d -> p (t d)").bitcast(I32))
 
         wg_first = keep.tile([P, PASSES * 2 * H], U8, name="wg_first", align_bytes=64)
         ident_src = sbuf_tile([P, P], F32, "ident_src", PLACE_LATE_LOADS)
@@ -147,7 +146,7 @@ def tile_moe_hie_none_kernel(
                     sc = sbuf_tile([P, count], U8, f"xg_scales{g}_{h}_{s}", PLACE_SCALES.get((g, h, s)))
                     nc.vector.tensor_copy(sc[:], x_plane[:, s * T : (s + 1) * T].indirect(entries))
                     w = sbuf_tile([P, count], U32, f"xg_words{g}_{h}_{s}", PLACE_WORDS.get((g, h, s)))
-                    nc.vector.tensor_copy(w[:], x_sb[:, s * T : (s + 1) * T].bitcast(U32).indirect(entries))
+                    nc.vector.tensor_copy(w[:], x_sb[s][:].bitcast(U32).indirect(entries))
                     for first in range(0, count, P):
                         scales.append(sc[:, first : first + P])
                         words.append(w[:, first : first + P])
@@ -239,32 +238,31 @@ def tile_moe_hie_none_kernel(
             return y_slots
 
         def scatter(g, y_slots):
-            entries = list_slice(dst_sb, g * C1, C1)
-            for t in range(4):
-                nc.vector.tensor_copy(y_win[t][:].indirect(entries), y_slots[:, t, :])
+            pieces = EPG if g == 0 else 1
+            count = C1 // pieces
+            for j in range(pieces):
+                entries = list_slice(dst_sb, g * C1 + j * count, count)
+                for t in range(4):
+                    nc.vector.tensor_copy(y_win[t][:].indirect(entries), y_slots[:, t, j * count : (j + 1) * count])
 
         tokens = [gather_tokens(g) for g in range(2)]
         first_layer(0, *tokens[0])
-        tokens.append(gather_tokens(2))
+        tokens += [gather_tokens(2), gather_tokens(3)]
         first_layer(1, *tokens[1])
         gate_turned = psum.tile([P, P], F32, name="gate_turned", offset=BANK * 7)
         nc.tensor.transpose(gate_turned[:], gate_rows[:], ident_f32[:])
         gate_col = keep.tile([P, E], F32, name="gate_col")
         nc.scalar.copy(gate_col[:], gate_turned[:, :E])
-        quantised0 = quantise(0, second_gather(0))
-        y0 = second_layer(0, *quantised0)
         first_layer(2, *tokens[2])
-        quantised1 = quantise(1, second_gather(1))
-        tokens3 = gather_tokens(3)
-        grouped2 = second_gather(2)
-        y1 = second_layer(1, *quantised1)
-        first_layer(3, *tokens3)
-        scatter(0, y0)
-        quantised2 = quantise(2, grouped2)
+        quantised = [quantise(g, second_gather(g)) for g in VECTOR_GROUPS]
+        y0 = second_layer(0, *quantised[0])
+        y1 = second_layer(1, *quantised[1])
+        first_layer(3, *tokens[3])
         grouped3 = second_gather(3)
-        y2 = second_layer(2, *quantised2)
-        scatter(1, y1)
+        scatter(0, y0)
         quantised3 = quantise(3, grouped3)
+        y2 = second_layer(2, *quantised[2])
+        scatter(1, y1)
         y3 = second_layer(3, *quantised3)
         scatter(2, y2)
         scatter(3, y3)

@@ -17,21 +17,32 @@ FP4X4 = mybir.dt.float4_e2m1fn_x4
 COPY = mybir.ActivationFunctionType.Copy
 
 P = 128
-PASSES = 2
-EPG = 2
-LIST_COLS = 16
-VECTOR_GROUPS = (0, 1, 2)
-FIRST_BANKS = ((0, 1, 4), (2, 3, 5), (0, 1, 6), (0, 1, 2))
-TURNED_BANKS = (1, 1, 1, 2)
+PACK = 4
+PASSES = K // (P * PACK)
+EPG = E // G
+PER_COLUMN = 16
+LAST = G - 1
+
+TOKEN_RUNS = ((0, P), (P, P), (C1, C1), (2 * C1, C1), (3 * C1, C1))
+EARLY_RUNS = 3
+OUT_PIECES = 4
+
 BANK = 2048
-PLACE_GROUPED = {}
-PLACE_Y_ROWS = {}
-PLACE_Y_SLOTS = {0: 6144}
-PLACE_CODES = {3: 6144}
-PLACE_WORDS = {(0, 0, 0): 768, (2, 0, 0): 0, (3, 0, 0): 1024, (0, 0, 1): 2816, (2, 0, 1): 2048, (3, 0, 1): 3072}
-PLACE_SCALES = {(0, 0, 0): 4288, (2, 0, 0): 4096, (3, 0, 0): 4352, (0, 0, 1): 4800, (2, 0, 1): 4608, (3, 0, 1): 4864}
-PLACE_LATE_LOADS = 14848
-SECOND_BANKS = ((1, 6, 4, 5), (4, 5, 0, 1), (2, 3, 4, 5), (4, 5, 6, 7))
+FIRST_BANKS = ((0, 1, 4), (2, 3, 5), (0, 1, 6), (2, 3, 0))
+SECOND_BANKS = ((1, 6, 4, 2), (4, 5, 1, 6), (4, 5, 1, 6), (2, 3, 0, 7))
+GATE_BANK = 7
+
+RUN_COLUMN = {
+    (0, 0): 0, (3, 0): 0, (0, 1): C1, (3, 1): C1,
+    (4, 0): 2 * C1, (4, 1): 3 * C1, (1, 1): 3 * C1 - P // 2,
+}
+PLACE_RUN_WORDS = 0
+PLACE_RUN_SCALES = PLACE_RUN_WORDS + PASSES * 2 * C1 * 4
+PLACE_FIRST_Y = PLACE_RUN_SCALES + PASSES * 2 * C1
+PLACE_LAST_WINDOW = PLACE_FIRST_Y + 4096
+PLACE_GATE = PLACE_LAST_WINDOW + 4096
+PLACE_IDENTITY = PLACE_GATE + 4 * C2 - 64
+PLACE_WEIGHTS = PLACE_IDENTITY + 64
 
 
 def tile_moe_hie_none_kernel(
@@ -49,44 +60,52 @@ def tile_moe_hie_none_kernel(
                 return keep.tile(shape, dtype, name=name, align_bytes=64)
             return placed.tile(shape, dtype, name=name, offset=place, align_bytes=64)
 
-        def load_scale_rows(queue, plane, rows, blocks):
+        def psum_tile(shape, dtype, name, bank):
+            return psum.tile(shape, dtype, name=name, offset=BANK * bank)
+
+        def load_list(entries, name):
+            tile = keep.tile([P, T // PER_COLUMN], U16, name=name)
+            nc.sync.dma_start(tile[:], entries)
+            return tile
+
+        def list_slice(tile, first, count):
+            return tile[:, first // PER_COLUMN : (first + count) // PER_COLUMN]
+
+        def load_scale_rows(plane, rows):
             by_row = rows.bitcast(I32).rearrange("s (q r) c -> r q s c", r=4)
             for r in range(4):
-                queue.dma_start(
-                    out=plane[r:P:32, :].bitcast(I32).rearrange("q (s c) -> q s c", s=blocks), in_=by_row[r]
-                )
+                target = plane[r:P:32, :].bitcast(I32).rearrange("q (s c) -> q s c", s=rows.shape[0])
+                nc.sync.dma_start(out=target, in_=by_row[r])
 
-        x_plane = keep.tile([P, PASSES * T], U8, name="x_plane", align_bytes=64)
-        wg_plane = keep.tile([P, G * PASSES * H], U8, name="wg_plane", align_bytes=64)
-        we_plane = keep.tile([P, E * N], U8, name="we_plane", align_bytes=64)
+        x_plane = sbuf_tile([P, PASSES * T], U8, "x_plane")
+        wg_plane = sbuf_tile([P, G * PASSES * H], U8, "wg_plane")
+        we_plane = sbuf_tile([P, E * N], U8, "we_plane")
         nc.vector.memset(x_plane[:].bitcast(I32), 0)
         nc.vector.memset(wg_plane[:].bitcast(I32), 0)
 
-        offs_sb = keep.tile([P, T // 16], U16, name="offs_sb")
-        nc.sync.dma_start(offs_sb[:], offs)
-        offs2_sb = keep.tile([P, T // 16], U16, name="offs2_sb")
-        nc.sync.dma_start(offs2_sb[:], offs2)
-        dst_sb = keep.tile([P, T // 16], U16, name="dst_sb")
-        nc.sync.dma_start(dst_sb[:], dst)
-        load_scale_rows(nc.sync, x_plane, x_scales, PASSES)
+        offs_sb = load_list(offs, "offs_sb")
+        offs2_sb = load_list(offs2, "offs2_sb")
+        dst_sb = load_list(dst, "dst_sb")
+        load_scale_rows(x_plane, x_scales)
         x_sb = []
         for s in range(PASSES):
-            x_sb.append(keep.tile([P, T], I32, name=f"x_sb{s}", align_bytes=64))
+            x_sb.append(sbuf_tile([P, T], I32, f"x_sb{s}"))
             nc.sync.dma_start(out=x_sb[s][:], in_=x_words[s].rearrange("p t d -> p (t d)").bitcast(I32))
 
-        wg_first = keep.tile([P, PASSES * 2 * H], U8, name="wg_first", align_bytes=64)
-        ident_src = sbuf_tile([P, P], F32, "ident_src", PLACE_LATE_LOADS)
-        make_identity(nc, ident_src[:])
+        ident_home = sbuf_tile([P, P], F32, "ident_home", PLACE_IDENTITY)
+        make_identity(nc, ident_home[:])
         nc.gpsimd.memset(we_plane[:].bitcast(I32), 0)
-        ident_f32 = keep.tile([P, P], F32, name="ident_f32")
-        ident_bf16 = keep.tile([P, P], BF16, name="ident_bf16")
-        nc.vector.tensor_copy(ident_f32[:], ident_src[:])
-        nc.vector.tensor_copy(ident_bf16[:], ident_src[:])
+        ident_f32 = sbuf_tile([P, P], F32, "ident_f32")
+        ident_bf16 = sbuf_tile([P, P], BF16, "ident_bf16")
+        nc.vector.tensor_copy(ident_f32[:], ident_home[:])
+        nc.scalar.activation(ident_bf16[:], ident_f32[:], COPY)
+
         wg_bytes, we_bytes = PASSES * 2 * H, EPG * 4 * N
-        weights = sbuf_tile([P, (G - 1) * wg_bytes + G * we_bytes], U8, "weights", PLACE_LATE_LOADS + 64)
-        wg_sb = [wg_first[:]] + [weights[:, g * wg_bytes : (g + 1) * wg_bytes] for g in range(G - 1)]
-        we_first = (G - 1) * wg_bytes
-        we_sb = [weights[:, we_first + g * we_bytes : we_first + (g + 1) * we_bytes] for g in range(G)]
+        wg_first = sbuf_tile([P, wg_bytes], U8, "wg_first")
+        later_weights = sbuf_tile([P, (G - 1) * wg_bytes + G * we_bytes], U8, "later_weights", PLACE_WEIGHTS)
+        wg_sb = [wg_first[:]] + [later_weights[:, g * wg_bytes : (g + 1) * wg_bytes] for g in range(G - 1)]
+        we_start = (G - 1) * wg_bytes
+        we_sb = [later_weights[:, we_start + g * we_bytes : we_start + (g + 1) * we_bytes] for g in range(G)]
 
         def load_wg(g):
             nc.sync.dma_start(
@@ -101,123 +120,108 @@ def tile_moe_hie_none_kernel(
             )
 
         load_wg(0)
-        load_scale_rows(nc.sync, wg_plane, wg_scales.rearrange("f s b c -> (f s) b c"), G * PASSES)
+        load_scale_rows(wg_plane, wg_scales.rearrange("f s b c -> (f s) b c"))
         load_wg(1)
-        gate_rows = sbuf_tile([P, C2], F32, "gate_rows", PLACE_LATE_LOADS + 64 - 4 * C2)
+        gate_rows = sbuf_tile([P, C2], F32, "gate_rows", PLACE_GATE)
         nc.sync.dma_start(out=gate_rows[:], in_=gate[: P // E, :].rearrange("r (e c) -> (r e) c", e=E))
         load_wg(2)
         load_we(0)
-        load_scale_rows(nc.sync, we_plane, we_scales.rearrange("e s b c -> (e s) b c"), E)
+        load_scale_rows(we_plane, we_scales.rearrange("e s b c -> (e s) b c"))
         load_we(1)
         load_wg(3)
         load_we(2)
         load_we(3)
-        warm = keep.tile([P, 1], F32, name="warm")
-        nc.scalar.activation(warm[:], ident_f32[:, 0:1], COPY)
 
         a_win = []
         for g in range(G):
-            if g in VECTOR_GROUPS:
-                planes, dtype, words = 2, F32, C1
+            planes = PACK if g == LAST else PACK // 2
+            columns = (planes + max(g, 1)) * C1
+            if g == LAST:
+                win = sbuf_tile([P, columns], BF16, f"a_win{g}", PLACE_LAST_WINDOW)
             else:
-                planes, dtype, words = 4, BF16, C1 // 2
-            tail = C1 if g == 0 else 0
-            win = keep.tile([P, g * C1 + planes * C1 + tail], dtype, name=f"a_win{g}", align_bytes=64)
-            if g == 0:
-                nc.vector.memset(win[:, planes * C1 :].bitcast(I32), 0)
-            else:
-                nc.vector.memset(win[:, : g * C1].bitcast(I32), 0)
+                win = sbuf_tile([P, columns], F32, f"a_win{g}")
+            spare = win[:, planes * C1 :] if g == 0 else win[:, : g * C1]
+            nc.vector.memset(spare.bitcast(I32), 0)
             a_win.append(win)
 
-        y_win = [keep.tile([P, T], F32, name=f"y_win{t}") for t in range(4)]
-        pairs = [keep.tile([P, 2, T // 2, 2], BF16, name=f"pairs{h}", align_bytes=64) for h in range(2)]
-        out_rows = out_0.rearrange("(p t) c -> p t c", t=4)
+        def gather_tokens(run):
+            first, count = TOKEN_RUNS[run]
+            entries = list_slice(offs_sb, first, count)
+            by_pass = []
+            for s in range(PASSES):
+                scales_place = words_place = None
+                if (run, s) in RUN_COLUMN:
+                    column = RUN_COLUMN[run, s]
+                    scales_place, words_place = PLACE_RUN_SCALES + column, PLACE_RUN_WORDS + 4 * column
+                scales = sbuf_tile([P, count], U8, f"run_scales{run}_{s}", scales_place)
+                nc.vector.tensor_copy(scales[:], x_plane[:, s * T : (s + 1) * T].indirect(entries))
+                words = sbuf_tile([P, count], U32, f"run_words{run}_{s}", words_place)
+                nc.vector.tensor_copy(words[:], x_sb[s][:].bitcast(U32).indirect(entries))
+                by_pass.append((words, scales))
+            return [[(w[:, c : c + P], z[:, c : c + P]) for w, z in by_pass] for c in range(0, count, P)]
 
-        def list_slice(tile, first, count):
-            return tile[:, first // 16 : (first + count) // 16]
-
-        def gather_tokens(g):
-            pieces = 2 if g == 0 else 1
-            count = C1 // pieces
-            words, scales = [], []
-            for h in range(pieces):
-                entries = list_slice(offs_sb, g * C1 + h * count, count)
-                for s in range(PASSES):
-                    sc = sbuf_tile([P, count], U8, f"xg_scales{g}_{h}_{s}", PLACE_SCALES.get((g, h, s)))
-                    nc.vector.tensor_copy(sc[:], x_plane[:, s * T : (s + 1) * T].indirect(entries))
-                    w = sbuf_tile([P, count], U32, f"xg_words{g}_{h}_{s}", PLACE_WORDS.get((g, h, s)))
-                    nc.vector.tensor_copy(w[:], x_sb[s][:].bitcast(U32).indirect(entries))
-                    for first in range(0, count, P):
-                        scales.append(sc[:, first : first + P])
-                        words.append(w[:, first : first + P])
-            order = [0, 1, 2, 3] if pieces == 2 else [0, 2, 1, 3]
-            return [words[i] for i in order], [scales[i] for i in order]
-
-        def first_layer(g, words, scales):
-            on_vector = g in VECTOR_GROUPS
-            planes = 2 if on_vector else 4
-            turned_banks = psum.tile(
-                [P, TURNED_BANKS[g] * planes, C1], F32 if on_vector else BF16, name=f"turned{g}", offset=BANK * FIRST_BANKS[g][2]
-            )
-            turned = turned_banks[:, :planes, :]
-            for h in range(2):
+        def first_layer(g, tokens):
+            planes = PACK if g == LAST else PACK // 2
+            turned = psum_tile([P, planes, C1], BF16 if g == LAST else F32, f"turned{g}", FIRST_BANKS[g][2])
+            for h in range(C1 // P):
                 cols = slice(h * P, (h + 1) * P)
-                acc = psum.tile([P, H], F32, name=f"acc1_{g}_{h}", offset=BANK * FIRST_BANKS[g][h])
-                for s in range(PASSES):
+                acc = psum_tile([P, H], F32, f"acc1_{g}_{h}", FIRST_BANKS[g][h])
+                for s, (words, scales) in enumerate(tokens[g * (C1 // P) + h]):
                     first = (g * PASSES + s) * H
                     nc.tensor.matmul_mx(
                         out=acc[:],
-                        lhsT=words[h * PASSES + s].bitcast(FP8X4),
-                        lhsT_scale=scales[h * PASSES + s],
+                        lhsT=words.bitcast(FP8X4),
+                        lhsT_scale=scales,
                         rhs=wg_sb[g][:, s * 2 * H : (s + 1) * 2 * H].bitcast(FP4X4),
                         rhs_scale=wg_plane[:, first : first + H],
                         start=(s == 0),
                         stop=(s == PASSES - 1),
                     )
                 a_rows = ring.tile([P, H], BF16, name="a_rows", align_bytes=64)
-                if on_vector:
+                if g == LAST:
+                    nc.scalar.copy(
+                        a_rows[:].rearrange("p (t m) -> p t m", t=PACK), acc[:].rearrange("p (m t) -> p t m", t=PACK)
+                    )
+                    for t in range(planes):
+                        nc.tensor.transpose(turned[:, t, cols], a_rows[:, t * P : (t + 1) * P], ident_bf16[:])
+                else:
                     nc.scalar.copy(
                         a_rows[:].rearrange("p (u m e) -> p u m e", u=2, e=2),
                         acc[:].rearrange("p (m u e) -> p u m e", u=2, e=2),
                     )
-                    for u in range(2):
-                        nc.tensor.transpose(turned[:, u, cols], a_rows[:].bitcast(F32)[:, u * P : (u + 1) * P], ident_f32[:])
-                else:
-                    nc.scalar.copy(
-                        a_rows[:].rearrange("p (t m) -> p t m", t=4), acc[:].rearrange("p (m t) -> p t m", t=4)
-                    )
-                    for t in range(4):
-                        nc.tensor.transpose(turned[:, t, cols], a_rows[:, t * P : (t + 1) * P], ident_bf16[:])
-            nc.scalar.copy(a_win[g][:, g * C1 : (g + planes) * C1], turned.rearrange("p t c -> p (t c)"))
+                    pair_words = a_rows[:].bitcast(F32)
+                    for u in range(planes):
+                        nc.tensor.transpose(turned[:, u, cols], pair_words[:, u * P : (u + 1) * P], ident_f32[:])
+            nc.scalar.copy(a_win[g][:, g * C1 : (g + planes) * C1], turned[:].rearrange("p t c -> p (t c)"))
 
         def second_gather(g):
             width = max(g + 1, 2) * C1
             entries = list_slice(offs2_sb, g * C1, C1)
-            grouped = sbuf_tile([P, C1 * 4], BF16, f"a_grouped{g}", PLACE_GROUPED.get(g))
-            if g in VECTOR_GROUPS:
-                target = grouped[:].bitcast(U32).rearrange("p (c u) -> p c u", u=2)
-                for u in range(2):
-                    window = a_win[g][:, u * C1 : u * C1 + width].bitcast(U32)
-                    nc.vector.tensor_copy(target[:, :, u], window.indirect(entries))
-            else:
-                target = grouped[:].rearrange("p (c t) -> p c t", t=4)
-                for t in range(4):
+            woven = sbuf_tile([P, C1 * PACK], BF16, f"a_woven{g}")
+            if g == LAST:
+                target = woven[:].rearrange("p (c t) -> p c t", t=PACK)
+                for t in range(PACK):
                     window = a_win[g][:, t * C1 : t * C1 + width]
                     nc.scalar.activation(target[:, :, t], window.indirect(entries), COPY)
-            return grouped
+            else:
+                target = woven[:].bitcast(U32).rearrange("p (c u) -> p c u", u=2)
+                for u in range(PACK // 2):
+                    window = a_win[g][:, u * C1 : u * C1 + width].bitcast(U32)
+                    nc.vector.tensor_copy(target[:, :, u], window.indirect(entries))
+            return woven
 
-        def quantise(g, grouped):
-            codes = sbuf_tile([P, C1], U32, f"a_codes{g}", PLACE_CODES.get(g))
-            scales = keep.tile([P, C1], U8, name=f"a_scales{g}", align_bytes=64)
-            nc.vector.quantize_mx(out=codes[:].bitcast(FP8X4), scales=scales[:], in_=grouped[:])
+        def quantise(g, woven):
+            codes = sbuf_tile([P, C1], U32, f"a_codes{g}", PLACE_FIRST_Y if g == LAST else None)
+            scales = sbuf_tile([P, C1], U8, f"a_scales{g}")
+            nc.vector.quantize_mx(out=codes[:].bitcast(FP8X4), scales=scales[:], in_=woven[:])
             return codes, scales
 
         def second_layer(g, codes, scales):
-            y_slots = sbuf_tile([P, 4, C1], F32, f"y_slots{g}", PLACE_Y_SLOTS.get(g))
+            y_slots = sbuf_tile([P, PACK, C1], F32, f"y_slots{g}", {0: PLACE_FIRST_Y, LAST - 1: PLACE_LAST_WINDOW}.get(g))
             for j in range(EPG):
                 e = g * EPG + j
                 cols = slice(j * C2, (j + 1) * C2)
-                acc = psum.tile([P, N], F32, name=f"acc2_{e}", offset=BANK * SECOND_BANKS[g][j])
+                acc = psum_tile([P, N], F32, f"acc2_{e}", SECOND_BANKS[g][j])
                 nc.tensor.matmul_mx(
                     out=acc[:],
                     lhsT=codes[:, cols].bitcast(FP8X4),
@@ -227,62 +231,80 @@ def tile_moe_hie_none_kernel(
                     start=True,
                     stop=True,
                 )
-                y_rows = sbuf_tile([P, 4, P], F32, f"y_rows{e}", PLACE_Y_ROWS.get(e))
+                y_rows = sbuf_tile([P, PACK, P], F32, f"y_rows{e}")
                 nc.scalar.activation(
-                    y_rows[:], acc[:].rearrange("p (m t) -> p t m", t=4), COPY, scale=gate_col[:, e : e + 1]
+                    y_rows[:], acc[:].rearrange("p (m t) -> p t m", t=PACK), COPY, scale=gate_col[:, e : e + 1]
                 )
-                back = psum.tile([P, 4, C2], F32, name=f"back{e}", offset=BANK * SECOND_BANKS[g][EPG + j])
-                for t in range(4):
+                banks = 2 if g == 0 else 1
+                back = psum_tile([P, banks * PACK, C2], F32, f"back{e}", SECOND_BANKS[g][EPG + j])
+                for t in range(PACK):
                     nc.tensor.transpose(back[:, t, :], y_rows[:, t, :], ident_f32[:])
-                nc.scalar.copy(y_slots[:, :, cols], back[:])
+                nc.scalar.copy(y_slots[:, :, cols], back[:, :PACK, :])
             return y_slots
 
-        def scatter(g, y_slots):
-            pieces = EPG if g == 0 else 1
-            count = C1 // pieces
-            for j in range(pieces):
-                entries = list_slice(dst_sb, g * C1 + j * count, count)
-                for t in range(4):
-                    nc.vector.tensor_copy(y_win[t][:].indirect(entries), y_slots[:, t, j * count : (j + 1) * count])
+        y_win = [keep.tile([P, T], F32, name=f"y_win{t}") for t in range(PACK)]
 
-        tokens = [gather_tokens(g) for g in range(2)]
-        first_layer(0, *tokens[0])
-        tokens += [gather_tokens(2), gather_tokens(3)]
-        first_layer(1, *tokens[1])
-        gate_turned = psum.tile([P, P], F32, name="gate_turned", offset=BANK * 7)
+        def scatter(g, y_slots):
+            count = C2 if g == 0 else C1
+            for first in range(0, C1, count):
+                entries = list_slice(dst_sb, g * C1 + first, count)
+                for t in range(PACK):
+                    nc.vector.tensor_copy(y_win[t][:].indirect(entries), y_slots[:, t, first : first + count])
+
+        tokens = []
+        for run in range(EARLY_RUNS):
+            tokens += gather_tokens(run)
+        first_layer(0, tokens)
+        for run in range(EARLY_RUNS, len(TOKEN_RUNS)):
+            tokens += gather_tokens(run)
+        first_layer(1, tokens)
+        gate_turned = psum_tile([P, P], F32, "gate_turned", GATE_BANK)
         nc.tensor.transpose(gate_turned[:], gate_rows[:], ident_f32[:])
-        gate_col = keep.tile([P, E], F32, name="gate_col")
+        gate_col = sbuf_tile([P, E], F32, "gate_col")
         nc.scalar.copy(gate_col[:], gate_turned[:, :E])
-        first_layer(2, *tokens[2])
-        quantised = [quantise(g, second_gather(g)) for g in VECTOR_GROUPS]
+        first_layer(2, tokens)
+        quantised = [quantise(g, second_gather(g)) for g in range(LAST)]
         y0 = second_layer(0, *quantised[0])
         y1 = second_layer(1, *quantised[1])
-        first_layer(3, *tokens[3])
-        grouped3 = second_gather(3)
+        first_layer(LAST, tokens)
+        woven_last = second_gather(LAST)
         scatter(0, y0)
-        quantised3 = quantise(3, grouped3)
+        quantised.append(quantise(LAST, woven_last))
         y2 = second_layer(2, *quantised[2])
         scatter(1, y1)
-        y3 = second_layer(3, *quantised3)
+        y3 = second_layer(LAST, *quantised[LAST])
         scatter(2, y2)
-        scatter(3, y3)
+        scatter(LAST, y3)
 
-        halves = [slice(0, T // 2), slice(T // 2, T)]
-        for t in range(4):
+        width = T // OUT_PIECES
+        pieces = [slice(k * width, (k + 1) * width) for k in range(OUT_PIECES)]
+        pairs = sbuf_tile([P, PACK * T], BF16, "pairs")
+        pair_view = pairs[:].rearrange("p (k u c e) -> p k u c e", k=OUT_PIECES, u=2, e=2)
+        out_rows = out_0.rearrange("(p t) c -> p t c", t=PACK)
+        for t in range(PACK):
             nc.sync.dma_start(out=out_rows[:, t, :], in_=y_win[t][:])
-            for h, cols in enumerate(halves):
-                nc.scalar.copy(pairs[h][:, t // 2, :, t % 2], y_win[t][:, cols])
-        out_codes = keep.tile([P, T], I32, name="out_codes", align_bytes=64)
-        out_plane = keep.tile([P, T], U8, name="out_plane", align_bytes=64)
+            if t < PACK - 1:
+                nc.scalar.copy(pair_view[:, :, t // 2, :, t % 2], y_win[t][:].rearrange("p (k c) -> p k c", k=OUT_PIECES))
+            else:
+                for k, cols in enumerate(pieces):
+                    nc.scalar.copy(pair_view[:, k, t // 2, :, t % 2], y_win[t][:, cols])
+        out_codes = sbuf_tile([P, T], I32, "out_codes")
+        out_plane = sbuf_tile([P, T], U8, "out_plane")
         code_rows = out_1[0].rearrange("p c d -> p (c d)").bitcast(I32)
-        for h, cols in enumerate(halves):
-            pair_words = pairs[h][:].rearrange("p u c e -> p u (c e)").bitcast(I32)
-            grouped = ring.tile([P, 2 * T], BF16, name="y_grouped", align_bytes=64)
-            nc.vector.tensor_copy(
-                grouped[:].bitcast(I32).rearrange("p (c u) -> p c u", u=2),
-                pair_words.rearrange("p u c -> p c u"),
-            )
-            nc.vector.quantize_mx(out=out_codes[:, cols].bitcast(FP8X4), scales=out_plane[:, cols], in_=grouped[:])
+        for k, cols in enumerate(pieces):
+            woven = sbuf_tile([P, width * PACK], BF16, f"y_woven{k}")
+            pair_rows = pairs[:, k * width * PACK : (k + 1) * width * PACK].rearrange("p (u w) -> p u w", u=2)
+            if k == OUT_PIECES - 1:
+                nc.scalar.copy(
+                    woven[:].bitcast(F32).rearrange("p (c u) -> p c u", u=2),
+                    pair_rows.bitcast(F32).rearrange("p u c -> p c u"),
+                )
+            else:
+                nc.vector.tensor_copy(
+                    woven[:].bitcast(I32).rearrange("p (c u) -> p c u", u=2),
+                    pair_rows.bitcast(I32).rearrange("p u c -> p c u"),
+                )
+            nc.vector.quantize_mx(out=out_codes[:, cols].bitcast(FP8X4), scales=out_plane[:, cols], in_=woven[:])
             nc.sync.dma_start(out=code_rows[:, cols], in_=out_codes[:, cols])
         scale_rows = out_2[0].bitcast(I32).rearrange("(q r) c -> r q c", r=4)
         for r in range(4):

from contextlib import ExitStack

import concourse.mybir as mybir
from concourse.masks import make_identity

K, T, G, C1, E, C2, H, N = 1024, 1024, 4, 256, 8, 128, 512, 512
FLOPS = 2 * K * H * T + 2 * H * N * T

F32 = mybir.dt.float32
BF16 = mybir.dt.bfloat16
I32 = mybir.dt.int32
U32 = mybir.dt.uint32
U16 = mybir.dt.uint16
U8 = mybir.dt.uint8
FP8X4 = mybir.dt.float8_e4m3fn_x4
FP4X4 = mybir.dt.float4_e2m1fn_x4
COPY = mybir.ActivationFunctionType.Copy

P = 128
PACK = 4
PASSES = K // (P * PACK)
EPG = E // G
PER_COLUMN = 16
LAST = G - 1

TOKEN_RUNS = ((0, P), (P, P), (C1, C1), (2 * C1, C1), (3 * C1, C1))
EARLY_RUNS = 3
OUT_PIECES = 4

BANK = 2048
FIRST_BANKS = ((0, 1, 4), (2, 3, 5), (0, 1, 6), (2, 3, 0))
SECOND_BANKS = ((1, 6, 4, 2), (4, 5, 1, 6), (4, 5, 1, 6), (2, 3, 0, 7))
GATE_BANK = 7

RUN_COLUMN = {
    (0, 0): 0, (3, 0): 0, (0, 1): C1, (3, 1): C1,
    (4, 0): 2 * C1, (4, 1): 3 * C1, (1, 1): 3 * C1 - P // 2,
}
PLACE_RUN_WORDS = 0
PLACE_RUN_SCALES = PLACE_RUN_WORDS + PASSES * 2 * C1 * 4
PLACE_FIRST_Y = PLACE_RUN_SCALES + PASSES * 2 * C1
PLACE_LAST_WINDOW = PLACE_FIRST_Y + 4096
PLACE_GATE = PLACE_LAST_WINDOW + 4096
PLACE_IDENTITY = PLACE_GATE + 4 * C2 - 64
PLACE_WEIGHTS = PLACE_IDENTITY + 64


def tile_moe_hie_none_kernel(
    tc, x_words, x_scales, wg_words, wg_scales, we_words, we_scales, gate, offs, offs2, dst, out_0, out_1, out_2
):
    nc = tc.nc
    with ExitStack() as ctx:
        keep = ctx.enter_context(tc.tile_pool(name="keep", bufs=1))
        ring = ctx.enter_context(tc.tile_pool(name="ring", bufs=2))
        placed = ctx.enter_context(tc.tile_pool(name="placed", bufs=1))
        psum = ctx.enter_context(tc.psum_pool(name="psum", bufs=1))

        def sbuf_tile(shape, dtype, name, place=None):
            if place is None:
                return keep.tile(shape, dtype, name=name, align_bytes=64)
            return placed.tile(shape, dtype, name=name, offset=place, align_bytes=64)

        def psum_tile(shape, dtype, name, bank):
            return psum.tile(shape, dtype, name=name, offset=BANK * bank)

        def load_list(entries, name):
            tile = keep.tile([P, T // PER_COLUMN], U16, name=name)
            nc.sync.dma_start(tile[:], entries)
            return tile

        def list_slice(tile, first, count):
            return tile[:, first // PER_COLUMN : (first + count) // PER_COLUMN]

        def load_scale_rows(plane, rows):
            by_row = rows.bitcast(I32).rearrange("s (q r) c -> r q s c", r=4)
            for r in range(4):
                target = plane[r:P:32, :].bitcast(I32).rearrange("q (s c) -> q s c", s=rows.shape[0])
                nc.sync.dma_start(out=target, in_=by_row[r])

        x_plane = sbuf_tile([P, PASSES * T], U8, "x_plane")
        wg_plane = sbuf_tile([P, G * PASSES * H], U8, "wg_plane")
        we_plane = sbuf_tile([P, E * N], U8, "we_plane")
        nc.vector.memset(x_plane[:].bitcast(I32), 0)
        nc.vector.memset(wg_plane[:].bitcast(I32), 0)

        offs_sb = load_list(offs, "offs_sb")
        offs2_sb = load_list(offs2, "offs2_sb")
        dst_sb = load_list(dst, "dst_sb")
        load_scale_rows(x_plane, x_scales)
        x_sb = []
        for s in range(PASSES):
            x_sb.append(sbuf_tile([P, T], I32, f"x_sb{s}"))
            nc.sync.dma_start(out=x_sb[s][:], in_=x_words[s].rearrange("p t d -> p (t d)").bitcast(I32))

        ident_home = sbuf_tile([P, P], F32, "ident_home", PLACE_IDENTITY)
        make_identity(nc, ident_home[:])
        nc.gpsimd.memset(we_plane[:].bitcast(I32), 0)
        ident_f32 = sbuf_tile([P, P], F32, "ident_f32")
        ident_bf16 = sbuf_tile([P, P], BF16, "ident_bf16")
        nc.vector.tensor_copy(ident_f32[:], ident_home[:])
        nc.scalar.activation(ident_bf16[:], ident_f32[:], COPY)

        wg_bytes, we_bytes = PASSES * 2 * H, EPG * 4 * N
        wg_first = sbuf_tile([P, wg_bytes], U8, "wg_first")
        later_weights = sbuf_tile([P, (G - 1) * wg_bytes + G * we_bytes], U8, "later_weights", PLACE_WEIGHTS)
        wg_sb = [wg_first[:]] + [later_weights[:, g * wg_bytes : (g + 1) * wg_bytes] for g in range(G - 1)]
        we_start = (G - 1) * wg_bytes
        we_sb = [later_weights[:, we_start + g * we_bytes : we_start + (g + 1) * we_bytes] for g in range(G)]

        def load_wg(g):
            nc.sync.dma_start(
                out=wg_sb[g].bitcast(I32).rearrange("p (s c) -> p s c", s=PASSES),
                in_=wg_words[g].bitcast(I32).rearrange("s p c -> p s c"),
            )

        def load_we(g):
            rows = we_words[EPG * g : EPG * (g + 1), 0].rearrange("e p n d -> e p (n d)").bitcast(I32)
            nc.sync.dma_start(
                out=we_sb[g].bitcast(I32).rearrange("p (e n) -> p e n", e=EPG), in_=rows.rearrange("e p n -> p e n")
            )

        load_wg(0)
        load_scale_rows(wg_plane, wg_scales.rearrange("f s b c -> (f s) b c"))
        load_wg(1)
        gate_rows = sbuf_tile([P, C2], F32, "gate_rows", PLACE_GATE)
        nc.sync.dma_start(out=gate_rows[:], in_=gate[: P // E, :].rearrange("r (e c) -> (r e) c", e=E))
        load_wg(2)
        load_we(0)
        load_scale_rows(we_plane, we_scales.rearrange("e s b c -> (e s) b c"))
        load_we(1)
        load_wg(3)
        load_we(2)
        load_we(3)

        a_win = []
        for g in range(G):
            planes = PACK if g == LAST else PACK // 2
            columns = (planes + max(g, 1)) * C1
            if g == LAST:
                win = sbuf_tile([P, columns], BF16, f"a_win{g}", PLACE_LAST_WINDOW)
            else:
                win = sbuf_tile([P, columns], F32, f"a_win{g}")
            spare = win[:, planes * C1 :] if g == 0 else win[:, : g * C1]
            nc.vector.memset(spare.bitcast(I32), 0)
            a_win.append(win)

        def gather_tokens(run):
            first, count = TOKEN_RUNS[run]
            entries = list_slice(offs_sb, first, count)
            by_pass = []
            for s in range(PASSES):
                scales_place = words_place = None
                if (run, s) in RUN_COLUMN:
                    column = RUN_COLUMN[run, s]
                    scales_place, words_place = PLACE_RUN_SCALES + column, PLACE_RUN_WORDS + 4 * column
                scales = sbuf_tile([P, count], U8, f"run_scales{run}_{s}", scales_place)
                nc.vector.tensor_copy(scales[:], x_plane[:, s * T : (s + 1) * T].indirect(entries))
                words = sbuf_tile([P, count], U32, f"run_words{run}_{s}", words_place)
                nc.vector.tensor_copy(words[:], x_sb[s][:].bitcast(U32).indirect(entries))
                by_pass.append((words, scales))
            return [[(w[:, c : c + P], z[:, c : c + P]) for w, z in by_pass] for c in range(0, count, P)]

        def first_layer(g, tokens):
            planes = PACK if g == LAST else PACK // 2
            turned = psum_tile([P, planes, C1], BF16 if g == LAST else F32, f"turned{g}", FIRST_BANKS[g][2])
            for h in range(C1 // P):
                cols = slice(h * P, (h + 1) * P)
                acc = psum_tile([P, H], F32, f"acc1_{g}_{h}", FIRST_BANKS[g][h])
                for s, (words, scales) in enumerate(tokens[g * (C1 // P) + h]):
                    first = (g * PASSES + s) * H
                    nc.tensor.matmul_mx(
                        out=acc[:],
                        lhsT=words.bitcast(FP8X4),
                        lhsT_scale=scales,
                        rhs=wg_sb[g][:, s * 2 * H : (s + 1) * 2 * H].bitcast(FP4X4),
                        rhs_scale=wg_plane[:, first : first + H],
                        start=(s == 0),
                        stop=(s == PASSES - 1),
                    )
                a_rows = ring.tile([P, H], BF16, name="a_rows", align_bytes=64)
                if g == LAST:
                    nc.scalar.copy(
                        a_rows[:].rearrange("p (t m) -> p t m", t=PACK), acc[:].rearrange("p (m t) -> p t m", t=PACK)
                    )
                    for t in range(planes):
                        nc.tensor.transpose(turned[:, t, cols], a_rows[:, t * P : (t + 1) * P], ident_bf16[:])
                else:
                    nc.scalar.copy(
                        a_rows[:].rearrange("p (u m e) -> p u m e", u=2, e=2),
                        acc[:].rearrange("p (m u e) -> p u m e", u=2, e=2),
                    )
                    pair_words = a_rows[:].bitcast(F32)
                    for u in range(planes):
                        nc.tensor.transpose(turned[:, u, cols], pair_words[:, u * P : (u + 1) * P], ident_f32[:])
            nc.scalar.copy(a_win[g][:, g * C1 : (g + planes) * C1], turned[:].rearrange("p t c -> p (t c)"))

        def second_gather(g):
            width = max(g + 1, 2) * C1
            entries = list_slice(offs2_sb, g * C1, C1)
            woven = sbuf_tile([P, C1 * PACK], BF16, f"a_woven{g}")
            if g == LAST:
                target = woven[:].rearrange("p (c t) -> p c t", t=PACK)
                for t in range(PACK):
                    window = a_win[g][:, t * C1 : t * C1 + width]
                    nc.scalar.activation(target[:, :, t], window.indirect(entries), COPY)
            else:
                target = woven[:].bitcast(U32).rearrange("p (c u) -> p c u", u=2)
                for u in range(PACK // 2):
                    window = a_win[g][:, u * C1 : u * C1 + width].bitcast(U32)
                    nc.vector.tensor_copy(target[:, :, u], window.indirect(entries))
            return woven

        def quantise(g, woven):
            codes = sbuf_tile([P, C1], U32, f"a_codes{g}", PLACE_FIRST_Y if g == LAST else None)
            scales = sbuf_tile([P, C1], U8, f"a_scales{g}")
            nc.vector.quantize_mx(out=codes[:].bitcast(FP8X4), scales=scales[:], in_=woven[:])
            return codes, scales

        def second_layer(g, codes, scales):
            y_slots = sbuf_tile([P, PACK, C1], F32, f"y_slots{g}", {0: PLACE_FIRST_Y, LAST - 1: PLACE_LAST_WINDOW}.get(g))
            for j in range(EPG):
                e = g * EPG + j
                cols = slice(j * C2, (j + 1) * C2)
                acc = psum_tile([P, N], F32, f"acc2_{e}", SECOND_BANKS[g][j])
                nc.tensor.matmul_mx(
                    out=acc[:],
                    lhsT=codes[:, cols].bitcast(FP8X4),
                    lhsT_scale=scales[:, cols],
                    rhs=we_sb[g][:, j * 4 * N : (j + 1) * 4 * N].bitcast(FP8X4),
                    rhs_scale=we_plane[:, e * N : (e + 1) * N],
                    start=True,
                    stop=True,
                )
                y_rows = sbuf_tile([P, PACK, P], F32, f"y_rows{e}")
                nc.scalar.activation(
                    y_rows[:], acc[:].rearrange("p (m t) -> p t m", t=PACK), COPY, scale=gate_col[:, e : e + 1]
                )
                banks = 2 if g == 0 else 1
                back = psum_tile([P, banks * PACK, C2], F32, f"back{e}", SECOND_BANKS[g][EPG + j])
                for t in range(PACK):
                    nc.tensor.transpose(back[:, t, :], y_rows[:, t, :], ident_f32[:])
                nc.scalar.copy(y_slots[:, :, cols], back[:, :PACK, :])
            return y_slots

        y_win = [keep.tile([P, T], F32, name=f"y_win{t}") for t in range(PACK)]

        def scatter(g, y_slots):
            count = C2 if g == 0 else C1
            for first in range(0, C1, count):
                entries = list_slice(dst_sb, g * C1 + first, count)
                for t in range(PACK):
                    nc.vector.tensor_copy(y_win[t][:].indirect(entries), y_slots[:, t, first : first + count])

        tokens = []
        for run in range(EARLY_RUNS):
            tokens += gather_tokens(run)
        first_layer(0, tokens)
        for run in range(EARLY_RUNS, len(TOKEN_RUNS)):
            tokens += gather_tokens(run)
        first_layer(1, tokens)
        gate_turned = psum_tile([P, P], F32, "gate_turned", GATE_BANK)
        nc.tensor.transpose(gate_turned[:], gate_rows[:], ident_f32[:])
        gate_col = sbuf_tile([P, E], F32, "gate_col")
        nc.scalar.copy(gate_col[:], gate_turned[:, :E])
        first_layer(2, tokens)
        quantised = [quantise(g, second_gather(g)) for g in range(LAST)]
        y0 = second_layer(0, *quantised[0])
        y1 = second_layer(1, *quantised[1])
        first_layer(LAST, tokens)
        woven_last = second_gather(LAST)
        scatter(0, y0)
        quantised.append(quantise(LAST, woven_last))
        y2 = second_layer(2, *quantised[2])
        scatter(1, y1)
        y3 = second_layer(LAST, *quantised[LAST])
        scatter(2, y2)
        scatter(LAST, y3)

        width = T // OUT_PIECES
        pieces = [slice(k * width, (k + 1) * width) for k in range(OUT_PIECES)]
        pairs = sbuf_tile([P, PACK * T], BF16, "pairs")
        pair_view = pairs[:].rearrange("p (k u c e) -> p k u c e", k=OUT_PIECES, u=2, e=2)
        out_rows = out_0.rearrange("(p t) c -> p t c", t=PACK)
        for t in range(PACK):
            nc.sync.dma_start(out=out_rows[:, t, :], in_=y_win[t][:])
            if t < PACK - 1:
                nc.scalar.copy(pair_view[:, :, t // 2, :, t % 2], y_win[t][:].rearrange("p (k c) -> p k c", k=OUT_PIECES))
            else:
                for k, cols in enumerate(pieces):
                    nc.scalar.copy(pair_view[:, k, t // 2, :, t % 2], y_win[t][:, cols])
        out_codes = sbuf_tile([P, T], I32, "out_codes")
        out_plane = sbuf_tile([P, T], U8, "out_plane")
        code_rows = out_1[0].rearrange("p c d -> p (c d)").bitcast(I32)
        for k, cols in enumerate(pieces):
            woven = sbuf_tile([P, width * PACK], BF16, f"y_woven{k}")
            pair_rows = pairs[:, k * width * PACK : (k + 1) * width * PACK].rearrange("p (u w) -> p u w", u=2)
            if k == OUT_PIECES - 1:
                nc.scalar.copy(
                    woven[:].bitcast(F32).rearrange("p (c u) -> p c u", u=2),
                    pair_rows.bitcast(F32).rearrange("p u c -> p c u"),
                )
            else:
                nc.vector.tensor_copy(
                    woven[:].bitcast(I32).rearrange("p (c u) -> p c u", u=2),
                    pair_rows.bitcast(I32).rearrange("p u c -> p c u"),
                )
            nc.vector.quantize_mx(out=out_codes[:, cols].bitcast(FP8X4), scales=out_plane[:, cols], in_=woven[:])
            nc.sync.dma_start(out=code_rows[:, cols], in_=out_codes[:, cols])
        scale_rows = out_2[0].bitcast(I32).rearrange("(q r) c -> r q c", r=4)
        for r in range(4):
            nc.scalar.dma_start(out=scale_rows[r], in_=out_plane[r:P:32, :].bitcast(I32))
